import numpy as np
import ml_dtypes


def mxq(x, axis, fmt="e4m3"):
    dtype, down = {"e4m3": (ml_dtypes.float8_e4m3fn, 7), "e5m2": (ml_dtypes.float8_e5m2, 14)}[fmt]
    v = np.moveaxis(np.asarray(x, np.float32).astype(ml_dtypes.bfloat16).astype(np.float64), axis, -1)
    blocks = v.reshape(v.shape[:-1] + (-1, 32))
    amax = np.abs(blocks).max(-1, keepdims=True)
    byte = np.maximum(np.where(amax > 0, np.frexp(amax)[1] - 1 + 127, 0) - down, 1)
    scale = np.exp2(byte - 127.0)
    codes = (blocks / scale).astype(np.float32).astype(dtype).astype(np.float64)
    return np.moveaxis((codes * scale).reshape(v.shape), -1, axis)


WIDE = False


def mx_kscale(k):
    if not WIDE:
        return np.ones(k)
    levels = np.array([30, -30])
    if k % 512:
        return np.exp2(np.random.permutation(np.resize(levels, k // 32))).repeat(32)
    a = np.empty((k // 512, 16))
    for p in range(k // 512):
        a[p, :8] = np.random.permutation(np.resize(levels, 8))
        for g in range(8):
            far = levels[np.abs(levels - a[p, g]) >= 10]
            a[p, g + 8] = far[np.random.randint(len(far))]
    return np.exp2(a.ravel()).repeat(32)


def f64(x):
    return np.asarray(x).astype(np.float64)


def striped(idx):
    return np.tile(np.asarray(idx).reshape(-1, 16).T, (8, 1)).astype(np.uint16)


def unstriped(offs):
    return offs[:16].T.reshape(-1).astype(np.int64)


E2M1 = np.array([0.0, 0.5, 1.0, 1.5, 2.0, 3.0, 4.0, 6.0, -0.0, -0.5, -1.0, -1.5, -2.0, -3.0, -4.0, -6.0])


def pack_weight(w, fmt):
    k, n = w.shape
    w = f64(np.asarray(w, np.float32).astype(ml_dtypes.bfloat16)).reshape(k // 32, 32, n)
    amax = np.abs(w).max(1)
    if fmt in ("e4m3", "e5m2"):
        byte = np.frexp(amax)[1] - 1 + 127 - (7 if fmt == "e4m3" else 14)
    else:
        mant, ex = np.frexp(amax / 6.0)
        byte = np.where(mant > 0.5, ex, ex - 1) + 127
    byte = np.clip(np.where(amax > 0, byte, 1), 1, 254)
    scaled = (w * np.exp2(127.0 - byte)[:, None, :]).reshape(k, n).astype(np.float32)
    by_word = np.ascontiguousarray(scaled.reshape(k // 512, 128, 4, n).transpose(0, 1, 3, 2))
    if fmt in ("e4m3", "e5m2"):
        words = by_word.astype(ml_dtypes.float8_e4m3fn if fmt == "e4m3" else ml_dtypes.float8_e5m2).view(np.uint8)
    else:
        c = by_word.astype(ml_dtypes.float4_e2m1fn).view(np.uint8) & 0xF
        words = (c[..., 0::2] | (c[..., 1::2] << 4)).reshape(k // 512, 128, 2 * n)
    return np.ascontiguousarray(words), np.ascontiguousarray(byte.astype(np.uint8).reshape(k // 512, 16, n))


def unpack_weight(words, scales, fmt):
    g, _, n = scales.shape
    words = np.ascontiguousarray(words).reshape(g, 128, n, -1)
    if fmt in ("e4m3", "e5m2"):
        vals = words.view(ml_dtypes.float8_e4m3fn if fmt == "e4m3" else ml_dtypes.float8_e5m2).astype(np.float64)
    else:
        nib = np.empty((g, 128, n, 4), np.uint8)
        nib[..., 0::2] = words & 0xF
        nib[..., 1::2] = words >> 4
        vals = E2M1[nib]
    vals = vals * np.repeat(np.exp2(scales.astype(np.float64) - 127.0), 8, axis=1)[..., None]
    return vals.transpose(0, 1, 3, 2).reshape(g * 512, n)


K, T, J, R, L, N = 512, 1024, 256, 512, 512, 256


def setup_inputs():
    n = np.random.standard_normal
    idx = np.random.permutation(T)[:J]
    fk = mx_kscale(K)
    fr = mx_kscale(R)
    fl = mx_kscale(L)
    xtp = pack_weight(n((K, T)) / fk[:, None], "e2m1")
    wp = pack_weight(n((K, R)) * 1 / np.sqrt(K) * fk[:, None] * fr, "e2m1")
    sxp = pack_weight(n((L, J)) / fl[:, None], "e4m3")
    wsp = pack_weight(n((L, R)) * 1 / np.sqrt(L) * fl[:, None] * fr, "e4m3")
    wbp = pack_weight(n((R, N)) * 1 / np.sqrt(R) / fr[:, None], "e5m2")
    return {
        "xt_words": xtp[0],
        "xt_scales": xtp[1],
        "w_words": wp[0],
        "w_scales": wp[1],
        "sx_words": sxp[0],
        "sx_scales": sxp[1],
        "ws_words": wsp[0],
        "ws_scales": wsp[1],
        "wb_words": wbp[0],
        "wb_scales": wbp[1],
        "rs": (1.0 * n((J, N))).astype(np.float32),
        "offs": striped(idx),
    }


def reference(xt_words, xt_scales, w_words, w_scales, sx_words, sx_scales, ws_words, ws_scales, wb_words, wb_scales, rs, offs):
    idx = unstriped(offs)
    xtu = unpack_weight(xt_words, xt_scales, "e2m1")
    wu = unpack_weight(w_words, w_scales, "e2m1")
    sxu = unpack_weight(sx_words, sx_scales, "e4m3")
    wsu = unpack_weight(ws_words, ws_scales, "e4m3")
    wbu = unpack_weight(wb_words, wb_scales, "e5m2")
    xtidxg = xtu[:, idx]
    a = wu.T @ xtidxg
    b2 = wsu.T @ sxu
    hid = np.maximum(a, b2)
    hidq = mxq(hid, 0, "e5m2")
    p = hidq.T @ wbu
    pk2 = np.max(np.abs(p), axis=1, keepdims=True)
    y = p / (pk2 + 0.2) + 0.3 * f64(rs)
    return y

@@ -1,0 +1,181 @@
+from contextlib import ExitStack
+
+import concourse.mybir as mybir
+
+K, T, J, R, L, N = 512, 1024, 256, 512, 512, 256
+FLOPS = 2 * K * R * J + 2 * L * R * J + 2 * R * J * N
+
+F32 = mybir.dt.float32
+BF16 = mybir.dt.bfloat16
+I32 = mybir.dt.int32
+U32 = mybir.dt.uint32
+U16 = mybir.dt.uint16
+U8 = mybir.dt.uint8
+E2M1 = mybir.dt.float4_e2m1fn_x4
+E4M3 = mybir.dt.float8_e4m3fn_x4
+E5M2 = mybir.dt.float8_e5m2_x4
+ALU = mybir.AluOpType
+ACT = mybir.ActivationFunctionType
+
+P = 128
+PACK = 4
+HALF = 128
+HALVES = J // HALF
+SECOND = 4
+
+
+def load_scale_rows(queues, plane, first, scales):
+    rows = scales[0].bitcast(I32)
+    for q in range(4):
+        start = 32 * q + first
+        queues[q].dma_start(out=plane[start : start + 4, :].bitcast(I32), in_=rows[4 * q : 4 * q + 4, :])
+
+
+def deal_columns(nc, dealt, source, run):
+    nc.vector.tensor_copy(
+        out=dealt.rearrange("p (t b i) -> p b t i", t=PACK, i=run),
+        in_=source.rearrange("p (b i t) -> p b t i", t=PACK, i=run),
+    )
+
+
+def tile_list_picked_rival_rowpeaks_kernel(
+    tc, xt_words, xt_scales, w_words, w_scales, sx_words, sx_scales, ws_words, ws_scales, wb_words, wb_scales, rs, offs, out
+):
+    nc = tc.nc
+    with ExitStack() as ctx:
+        sb = ctx.enter_context(tc.tile_pool(name="sb", bufs=1))
+        ps = ctx.enter_context(tc.psum_pool(name="ps", bufs=1))
+
+        offsets = sb.tile([P, J // 16], U16, name="offsets")
+        xt_w = sb.tile([P, T], U16, name="xt_w", align_bytes=64)
+        xt_s = sb.tile([P, T], U8, name="xt_s", align_bytes=64)
+        w_w = sb.tile([P, R], U16, name="w_w", tag="narrow_words", align_bytes=64)
+        ws_w = sb.tile([P, R], U32, name="ws_w", tag="wide_rows", align_bytes=64)
+        first_s = sb.tile([P, R], U8, name="first_s", align_bytes=64)
+        sx_w = sb.tile([P, J], U32, name="sx_w", align_bytes=64)
+        sx_s = sb.tile([P, J], U8, name="sx_s", align_bytes=64)
+
+        nc.gpsimd.memset(xt_s[:].bitcast(I32), 0)
+        nc.vector.memset(first_s[:].bitcast(I32), 0)
+        nc.vector.memset(sx_s[:].bitcast(I32), 0)
+
+        def words(dram):
+            return dram[0].rearrange("p c t -> p (c t)").bitcast(I32)
+
+        nc.sync.dma_start(offsets[:], offs)
+        nc.scalar.dma_start(out=xt_w[:].bitcast(I32), in_=xt_words[0].bitcast(I32))
+        nc.sync.dma_start(out=w_w[:].bitcast(I32), in_=w_words[0].bitcast(I32))
+        nc.scalar.dma_start(out=ws_w[:].bitcast(I32), in_=words(ws_words))
+        load_scale_rows((nc.sync, nc.scalar, nc.sync, nc.scalar), xt_s, 0, xt_scales)
+        load_scale_rows((nc.sync, nc.scalar, nc.sync, nc.scalar), first_s, 0, w_scales)
+        load_scale_rows((nc.sync, nc.scalar, nc.sync, nc.scalar), first_s, SECOND, ws_scales)
+        nc.gpsimd.dma_start(out=sx_w[:].bitcast(I32), in_=words(sx_words))
+        load_scale_rows((nc.gpsimd, nc.gpsimd, nc.sync, nc.sync), sx_s, 0, sx_scales)
+
+        picks = []
+        for h in range(HALVES):
+            entries = offsets[:, h * HALF // 16 : (h + 1) * HALF // 16]
+            pick_w = sb.tile([P, HALF], U16, name=f"pick_w{h}", align_bytes=64)
+            pick_s = sb.tile([P, HALF], U8, name=f"pick_s{h}", align_bytes=64)
+            nc.vector.tensor_copy(out=pick_w[:], in_=xt_w[:].indirect(entries))
+            nc.vector.tensor_copy(out=pick_s[:], in_=xt_s[:].indirect(entries))
+            picks.append((pick_w, pick_s))
+
+        ws_wd = sb.tile([P, R], U32, name="ws_wd", align_bytes=64)
+        w_wd = sb.tile([P, R], U16, name="w_wd", align_bytes=64)
+        first_sd = sb.tile([P, R], U8, name="first_sd", align_bytes=64)
+        deal_columns(nc, w_wd[:], w_w[:], 8)
+        deal_columns(nc, ws_wd[:], ws_w[:], 4)
+        deal_columns(nc, first_sd[:], first_s[:], 16)
+
+        wb_w = sb.tile([P, N], U32, name="wb_w", tag="narrow_words", align_bytes=64)
+        res = sb.tile([P, HALVES, N], F32, name="res", tag="wide_rows", align_bytes=64)
+        wb_s = first_s[:, 0:N]
+        nc.sync.dma_start(out=wb_w[:].bitcast(I32), in_=words(wb_words))
+        nc.sync.dma_start(out=res[:], in_=rs.rearrange("(h p) n -> p h n", p=P))
+        load_scale_rows((nc.sync, nc.sync, nc.sync, nc.sync), wb_s, 0, wb_scales)
+
+        picked = []
+        for h in range(HALVES):
+            pick_w, pick_s = picks[h]
+            bank = ps.tile([P, PACK, HALF], F32, name=f"tok_bank{h}")
+            for t in range(PACK):
+                rows = slice(t * P, (t + 1) * P)
+                nc.tensor.matmul_mx(
+                    out=bank[:, t, :],
+                    lhsT=w_wd[:, rows].bitcast(E2M1),
+                    lhsT_scale=first_sd[:, rows],
+                    rhs=pick_w[:].bitcast(E2M1),
+                    rhs_scale=pick_s[:],
+                    start=True,
+                    stop=True,
+                )
+            woven = sb.tile([P, HALF, PACK], F32, name=f"tok{h}")
+            nc.scalar.copy(out=woven[:], in_=bank[:].rearrange("p t j -> p j t"))
+            picked.append(woven)
+
+        res_scaled = sb.tile([P, HALVES, N], F32, name="res_scaled")
+        nc.scalar.activation(out=res_scaled[:], in_=res[:], func=ACT.Copy, scale=0.3)
+
+        own = []
+        for h in range(HALVES):
+            cols = slice(h * HALF, (h + 1) * HALF)
+            bank = ps.tile([P, PACK, HALF], F32, name=f"own_bank{h}")
+            for t in range(PACK):
+                rows = slice(t * P, (t + 1) * P)
+                nc.tensor.matmul_mx(
+                    out=bank[:, t, :],
+                    lhsT=ws_wd[:, rows].bitcast(E4M3),
+                    lhsT_scale=first_sd[SECOND:, rows],
+                    rhs=sx_w[:, cols].bitcast(E4M3),
+                    rhs_scale=sx_s[:, cols],
+                    start=True,
+                    stop=True,
+                )
+            own.append(bank)
+
+        hid = []
+        for h in range(HALVES):
+            rounded = sb.tile([P, HALF, PACK], BF16, name=f"hid{h}", align_bytes=64)
+            nc.vector.tensor_tensor(out=rounded[:], in0=own[h][:].rearrange("p t j -> p j t"), in1=picked[h][:], op=ALU.max)
+            hid.append(rounded)
+
+        second = []
+        for h in range(HALVES):
+            hid_w = sb.tile([P, HALF], U32, name=f"hid_w{h}", align_bytes=64)
+            hid_s = sb.tile([P, HALF], U8, name=f"hid_s{h}", align_bytes=64)
+            nc.vector.quantize_mx(out=hid_w[:].bitcast(E5M2), scales=hid_s[:], in_=hid[h][:].rearrange("p j t -> p (j t)"))
+            bank = ps.tile([P, N], F32, name=f"out_bank{h}")
+            nc.tensor.matmul_mx(
+                out=bank[:],
+                lhsT=hid_w[:].bitcast(E5M2),
+                lhsT_scale=hid_s[:],
+                rhs=wb_w[:].bitcast(E5M2),
+                rhs_scale=wb_s,
+                start=True,
+                stop=True,
+            )
+            second.append(bank)
+
+        peaks = []
+        for h in range(HALVES):
+            size = sb.tile([P, N], F32, name=f"size{h}")
+            nc.scalar.activation(out=size[:], in_=second[h][:], func=ACT.Abs)
+            peak = sb.tile([P, 1], F32, name=f"peak{h}")
+            nc.vector.tensor_scalar(
+                out=size[:], in0=size[:], scalar1=0.2, scalar2=None, op0=ALU.add, op1=ALU.max, accum_out=peak[:]
+            )
+            peaks.append(peak)
+
+        inverses = []
+        for h in range(HALVES):
+            inverse = sb.tile([P, 1], F32, name=f"inverse{h}")
+            nc.vector.reciprocal(out=inverse[:], in_=peaks[h][:])
+            inverses.append(inverse)
+
+        for h, queue in enumerate((nc.sync, nc.scalar)):
+            result = sb.tile([P, N], F32, name=f"result{h}")
+            nc.vector.scalar_tensor_tensor(
+                out=result[:], in0=second[h][:], scalar=inverses[h][:], in1=res_scaled[:, h, :], op0=ALU.mult, op1=ALU.add
+            )
+            queue.dma_start(out=out[h * HALF : (h + 1) * HALF, :], in_=result[:])

@@ -21,14 +21,21 @@ P = 128
 PACK = 4
 HALF = 128
 HALVES = J // HALF
-SECOND = 4
 
 
-def load_scale_rows(queues, plane, first, scales):
+def load_scale_rows(queues, plane, scales):
     rows = scales[0].bitcast(I32)
     for q in range(4):
-        start = 32 * q + first
-        queues[q].dma_start(out=plane[start : start + 4, :].bitcast(I32), in_=rows[4 * q : 4 * q + 4, :])
+        queues[q].dma_start(out=plane[32 * q : 32 * q + 4, :].bitcast(I32), in_=rows[4 * q : 4 * q + 4, :])
+
+
+def load_scale_rows_repeated(queues, plane, scales):
+    rows = scales[0].bitcast(I32)
+    for q in range(4):
+        four = rows[4 * q : 4 * q + 4, :]
+        queues[q].dma_start(
+            out=plane[32 * q : 32 * q + 32, :].bitcast(I32), in_=four.unsqueeze(0).broadcast_to([8, 4, rows.shape[1]])
+        )
 
 
 def deal_columns(nc, dealt, source, run):
@@ -51,62 +58,63 @@ def tile_list_picked_rival_rowpeaks_kernel(
         xt_s = sb.tile([P, T], U8, name="xt_s", align_bytes=64)
         w_w = sb.tile([P, R], U16, name="w_w", tag="narrow_words", align_bytes=64)
         ws_w = sb.tile([P, R], U32, name="ws_w", tag="wide_rows", align_bytes=64)
-        first_s = sb.tile([P, R], U8, name="first_s", align_bytes=64)
+        w_s = sb.tile([P, R], U8, name="w_s", align_bytes=64)
+        ws_s = sb.tile([P, R], U8, name="ws_s", align_bytes=64)
         sx_w = sb.tile([P, J], U32, name="sx_w", align_bytes=64)
         sx_s = sb.tile([P, J], U8, name="sx_s", align_bytes=64)
 
         nc.gpsimd.memset(xt_s[:].bitcast(I32), 0)
-        nc.vector.memset(first_s[:].bitcast(I32), 0)
+        nc.vector.memset(ws_s[:].bitcast(I32), 0)
         nc.vector.memset(sx_s[:].bitcast(I32), 0)
 
         def words(dram):
             return dram[0].rearrange("p c t -> p (c t)").bitcast(I32)
 
+        both = (nc.sync, nc.scalar, nc.sync, nc.scalar)
+        load_scale_rows_repeated(both, w_s, w_scales)
         nc.sync.dma_start(offsets[:], offs)
         nc.scalar.dma_start(out=xt_w[:].bitcast(I32), in_=xt_words[0].bitcast(I32))
         nc.sync.dma_start(out=w_w[:].bitcast(I32), in_=w_words[0].bitcast(I32))
         nc.scalar.dma_start(out=ws_w[:].bitcast(I32), in_=words(ws_words))
-        load_scale_rows((nc.sync, nc.scalar, nc.sync, nc.scalar), xt_s, 0, xt_scales)
-        load_scale_rows((nc.sync, nc.scalar, nc.sync, nc.scalar), first_s, 0, w_scales)
-        load_scale_rows((nc.sync, nc.scalar, nc.sync, nc.scalar), first_s, SECOND, ws_scales)
-        nc.gpsimd.dma_start(out=sx_w[:].bitcast(I32), in_=words(sx_words))
-        load_scale_rows((nc.gpsimd, nc.gpsimd, nc.sync, nc.sync), sx_s, 0, sx_scales)
-
-        picks = []
-        for h in range(HALVES):
-            entries = offsets[:, h * HALF // 16 : (h + 1) * HALF // 16]
-            pick_w = sb.tile([P, HALF], U16, name=f"pick_w{h}", align_bytes=64)
-            pick_s = sb.tile([P, HALF], U8, name=f"pick_s{h}", align_bytes=64)
-            nc.vector.tensor_copy(out=pick_w[:], in_=xt_w[:].indirect(entries))
-            nc.vector.tensor_copy(out=pick_s[:], in_=xt_s[:].indirect(entries))
-            picks.append((pick_w, pick_s))
+        load_scale_rows(both, xt_s, xt_scales)
+        load_scale_rows([nc.sync] * 4, ws_s, ws_scales)
+        load_scale_rows([nc.sync] * 4, sx_s, sx_scales)
+        nc.sync.dma_start(out=sx_w[:].bitcast(I32), in_=words(sx_words))
 
         ws_wd = sb.tile([P, R], U32, name="ws_wd", align_bytes=64)
+        ws_sd = sb.tile([P, R], U8, name="ws_sd", align_bytes=64)
         w_wd = sb.tile([P, R], U16, name="w_wd", align_bytes=64)
-        first_sd = sb.tile([P, R], U8, name="first_sd", align_bytes=64)
+        w_sd = sb.tile([P, R], U8, name="w_sd", align_bytes=64)
+        deal_columns(nc, w_sd[:], w_s[:], 16)
+        entries = [offsets[:, h * HALF // 16 : (h + 1) * HALF // 16] for h in range(HALVES)]
+        pick_w = [sb.tile([P, HALF], U16, name=f"pick_w{h}", align_bytes=64) for h in range(HALVES)]
+        pick_s = [sb.tile([P, HALF], U8, name=f"pick_s{h}", align_bytes=64) for h in range(HALVES)]
+        for h in range(HALVES):
+            nc.vector.tensor_copy(out=pick_w[h][:], in_=xt_w[:].indirect(entries[h]))
         deal_columns(nc, w_wd[:], w_w[:], 8)
         deal_columns(nc, ws_wd[:], ws_w[:], 4)
-        deal_columns(nc, first_sd[:], first_s[:], 16)
+        for h in range(HALVES):
+            nc.vector.tensor_copy(out=pick_s[h][:], in_=xt_s[:].indirect(entries[h]))
+        deal_columns(nc, ws_sd[:], ws_s[:], 16)
 
         wb_w = sb.tile([P, N], U32, name="wb_w", tag="narrow_words", align_bytes=64)
         res = sb.tile([P, HALVES, N], F32, name="res", tag="wide_rows", align_bytes=64)
-        wb_s = first_s[:, 0:N]
+        wb_s = ws_s[:, 0:N]
         nc.sync.dma_start(out=wb_w[:].bitcast(I32), in_=words(wb_words))
         nc.sync.dma_start(out=res[:], in_=rs.rearrange("(h p) n -> p h n", p=P))
-        load_scale_rows((nc.sync, nc.sync, nc.sync, nc.sync), wb_s, 0, wb_scales)
+        load_scale_rows([nc.sync] * 4, wb_s, wb_scales)
 
         picked = []
         for h in range(HALVES):
-            pick_w, pick_s = picks[h]
             bank = ps.tile([P, PACK, HALF], F32, name=f"tok_bank{h}")
             for t in range(PACK):
                 rows = slice(t * P, (t + 1) * P)
                 nc.tensor.matmul_mx(
                     out=bank[:, t, :],
                     lhsT=w_wd[:, rows].bitcast(E2M1),
-                    lhsT_scale=first_sd[:, rows],
-                    rhs=pick_w[:].bitcast(E2M1),
-                    rhs_scale=pick_s[:],
+                    lhsT_scale=w_sd[:, rows],
+                    rhs=pick_w[h][:].bitcast(E2M1),
+                    rhs_scale=pick_s[h][:],
                     start=True,
                     stop=True,
                 )
@@ -126,7 +134,7 @@ def tile_list_picked_rival_rowpeaks_kernel(
                 nc.tensor.matmul_mx(
                     out=bank[:, t, :],
                     lhsT=ws_wd[:, rows].bitcast(E4M3),
-                    lhsT_scale=first_sd[SECOND:, rows],
+                    lhsT_scale=ws_sd[:, rows],
                     rhs=sx_w[:, cols].bitcast(E4M3),
                     rhs_scale=sx_s[:, cols],
                     start=True,

from contextlib import ExitStack

import concourse.mybir as mybir

K, T, J, R, L, N = 512, 1024, 256, 512, 512, 256
FLOPS = 2 * K * R * J + 2 * L * R * J + 2 * R * J * N

F32 = mybir.dt.float32
BF16 = mybir.dt.bfloat16
I32 = mybir.dt.int32
U32 = mybir.dt.uint32
U16 = mybir.dt.uint16
U8 = mybir.dt.uint8
E2M1 = mybir.dt.float4_e2m1fn_x4
E4M3 = mybir.dt.float8_e4m3fn_x4
E5M2 = mybir.dt.float8_e5m2_x4
ALU = mybir.AluOpType
ACT = mybir.ActivationFunctionType

P = 128
PACK = 4
HALF = 128
HALVES = J // HALF


def load_scale_rows(queues, plane, scales):
    rows = scales[0].bitcast(I32)
    for q in range(4):
        queues[q].dma_start(out=plane[32 * q : 32 * q + 4, :].bitcast(I32), in_=rows[4 * q : 4 * q + 4, :])


def load_scale_rows_repeated(queues, plane, scales):
    rows = scales[0].bitcast(I32)
    for q in range(4):
        four = rows[4 * q : 4 * q + 4, :]
        queues[q].dma_start(
            out=plane[32 * q : 32 * q + 32, :].bitcast(I32), in_=four.unsqueeze(0).broadcast_to([8, 4, rows.shape[1]])
        )


def deal_columns(nc, dealt, source, run):
    nc.vector.tensor_copy(
        out=dealt.rearrange("p (t b i) -> p b t i", t=PACK, i=run),
        in_=source.rearrange("p (b i t) -> p b t i", t=PACK, i=run),
    )


def tile_list_picked_rival_rowpeaks_kernel(
    tc, xt_words, xt_scales, w_words, w_scales, sx_words, sx_scales, ws_words, ws_scales, wb_words, wb_scales, rs, offs, out
):
    nc = tc.nc
    with ExitStack() as ctx:
        sb = ctx.enter_context(tc.tile_pool(name="sb", bufs=1))
        ps = ctx.enter_context(tc.psum_pool(name="ps", bufs=1))

        offsets = sb.tile([P, J // 16], U16, name="offsets")
        xt_w = sb.tile([P, T], U16, name="xt_w", align_bytes=64)
        xt_s = sb.tile([P, T], U8, name="xt_s", align_bytes=64)
        w_w = sb.tile([P, R], U16, name="w_w", tag="narrow_words", align_bytes=64)
        ws_w = sb.tile([P, R], U32, name="ws_w", tag="wide_rows", align_bytes=64)
        w_s = sb.tile([P, R], U8, name="w_s", align_bytes=64)
        ws_s = sb.tile([P, R], U8, name="ws_s", align_bytes=64)
        sx_w = sb.tile([P, J], U32, name="sx_w", align_bytes=64)
        sx_s = sb.tile([P, J], U8, name="sx_s", align_bytes=64)

        nc.gpsimd.memset(xt_s[:].bitcast(I32), 0)
        nc.vector.memset(ws_s[:].bitcast(I32), 0)
        nc.vector.memset(sx_s[:].bitcast(I32), 0)

        def words(dram):
            return dram[0].rearrange("p c t -> p (c t)").bitcast(I32)

        both = (nc.sync, nc.scalar, nc.sync, nc.scalar)
        load_scale_rows_repeated(both, w_s, w_scales)
        nc.sync.dma_start(offsets[:], offs)
        nc.scalar.dma_start(out=xt_w[:].bitcast(I32), in_=xt_words[0].bitcast(I32))
        nc.sync.dma_start(out=w_w[:].bitcast(I32), in_=w_words[0].bitcast(I32))
        nc.scalar.dma_start(out=ws_w[:].bitcast(I32), in_=words(ws_words))
        load_scale_rows(both, xt_s, xt_scales)
        load_scale_rows([nc.sync] * 4, ws_s, ws_scales)
        load_scale_rows([nc.sync] * 4, sx_s, sx_scales)
        nc.sync.dma_start(out=sx_w[:].bitcast(I32), in_=words(sx_words))

        ws_wd = sb.tile([P, R], U32, name="ws_wd", align_bytes=64)
        ws_sd = sb.tile([P, R], U8, name="ws_sd", align_bytes=64)
        w_wd = sb.tile([P, R], U16, name="w_wd", align_bytes=64)
        w_sd = sb.tile([P, R], U8, name="w_sd", align_bytes=64)
        deal_columns(nc, w_sd[:], w_s[:], 16)
        entries = [offsets[:, h * HALF // 16 : (h + 1) * HALF // 16] for h in range(HALVES)]
        pick_w = [sb.tile([P, HALF], U16, name=f"pick_w{h}", align_bytes=64) for h in range(HALVES)]
        pick_s = [sb.tile([P, HALF], U8, name=f"pick_s{h}", align_bytes=64) for h in range(HALVES)]
        for h in range(HALVES):
            nc.vector.tensor_copy(out=pick_w[h][:], in_=xt_w[:].indirect(entries[h]))
        deal_columns(nc, w_wd[:], w_w[:], 8)
        deal_columns(nc, ws_wd[:], ws_w[:], 4)
        for h in range(HALVES):
            nc.vector.tensor_copy(out=pick_s[h][:], in_=xt_s[:].indirect(entries[h]))
        deal_columns(nc, ws_sd[:], ws_s[:], 16)

        wb_w = sb.tile([P, N], U32, name="wb_w", tag="narrow_words", align_bytes=64)
        res = sb.tile([P, HALVES, N], F32, name="res", tag="wide_rows", align_bytes=64)
        wb_s = ws_s[:, 0:N]
        nc.sync.dma_start(out=wb_w[:].bitcast(I32), in_=words(wb_words))
        nc.sync.dma_start(out=res[:], in_=rs.rearrange("(h p) n -> p h n", p=P))
        load_scale_rows([nc.sync] * 4, wb_s, wb_scales)

        picked = []
        for h in range(HALVES):
            bank = ps.tile([P, PACK, HALF], F32, name=f"tok_bank{h}")
            for t in range(PACK):
                rows = slice(t * P, (t + 1) * P)
                nc.tensor.matmul_mx(
                    out=bank[:, t, :],
                    lhsT=w_wd[:, rows].bitcast(E2M1),
                    lhsT_scale=w_sd[:, rows],
                    rhs=pick_w[h][:].bitcast(E2M1),
                    rhs_scale=pick_s[h][:],
                    start=True,
                    stop=True,
                )
            woven = sb.tile([P, HALF, PACK], F32, name=f"tok{h}")
            nc.scalar.copy(out=woven[:], in_=bank[:].rearrange("p t j -> p j t"))
            picked.append(woven)

        res_scaled = sb.tile([P, HALVES, N], F32, name="res_scaled")
        nc.scalar.activation(out=res_scaled[:], in_=res[:], func=ACT.Copy, scale=0.3)

        own = []
        for h in range(HALVES):
            cols = slice(h * HALF, (h + 1) * HALF)
            bank = ps.tile([P, PACK, HALF], F32, name=f"own_bank{h}")
            for t in range(PACK):
                rows = slice(t * P, (t + 1) * P)
                nc.tensor.matmul_mx(
                    out=bank[:, t, :],
                    lhsT=ws_wd[:, rows].bitcast(E4M3),
                    lhsT_scale=ws_sd[:, rows],
                    rhs=sx_w[:, cols].bitcast(E4M3),
                    rhs_scale=sx_s[:, cols],
                    start=True,
                    stop=True,
                )
            own.append(bank)

        hid = []
        for h in range(HALVES):
            rounded = sb.tile([P, HALF, PACK], BF16, name=f"hid{h}", align_bytes=64)
            nc.vector.tensor_tensor(out=rounded[:], in0=own[h][:].rearrange("p t j -> p j t"), in1=picked[h][:], op=ALU.max)
            hid.append(rounded)

        second = []
        for h in range(HALVES):
            hid_w = sb.tile([P, HALF], U32, name=f"hid_w{h}", align_bytes=64)
            hid_s = sb.tile([P, HALF], U8, name=f"hid_s{h}", align_bytes=64)
            nc.vector.quantize_mx(out=hid_w[:].bitcast(E5M2), scales=hid_s[:], in_=hid[h][:].rearrange("p j t -> p (j t)"))
            bank = ps.tile([P, N], F32, name=f"out_bank{h}")
            nc.tensor.matmul_mx(
                out=bank[:],
                lhsT=hid_w[:].bitcast(E5M2),
                lhsT_scale=hid_s[:],
                rhs=wb_w[:].bitcast(E5M2),
                rhs_scale=wb_s,
                start=True,
                stop=True,
            )
            second.append(bank)

        peaks = []
        for h in range(HALVES):
            size = sb.tile([P, N], F32, name=f"size{h}")
            nc.scalar.activation(out=size[:], in_=second[h][:], func=ACT.Abs)
            peak = sb.tile([P, 1], F32, name=f"peak{h}")
            nc.vector.tensor_scalar(
                out=size[:], in0=size[:], scalar1=0.2, scalar2=None, op0=ALU.add, op1=ALU.max, accum_out=peak[:]
            )
            peaks.append(peak)

        inverses = []
        for h in range(HALVES):
            inverse = sb.tile([P, 1], F32, name=f"inverse{h}")
            nc.vector.reciprocal(out=inverse[:], in_=peaks[h][:])
            inverses.append(inverse)

        for h, queue in enumerate((nc.sync, nc.scalar)):
            result = sb.tile([P, N], F32, name=f"result{h}")
            nc.vector.scalar_tensor_tensor(
                out=result[:], in0=second[h][:], scalar=inverses[h][:], in1=res_scaled[:, h, :], op0=ALU.mult, op1=ALU.add
            )
            queue.dma_start(out=out[h * HALF : (h + 1) * HALF, :], in_=result[:])
